import numpy as np
import ml_dtypes


def mxq(x, axis, fmt="e4m3"):
    dtype, down = {"e4m3": (ml_dtypes.float8_e4m3fn, 7), "e5m2": (ml_dtypes.float8_e5m2, 14)}[fmt]
    v = np.moveaxis(np.asarray(x, np.float32).astype(ml_dtypes.bfloat16).astype(np.float64), axis, -1)
    blocks = v.reshape(v.shape[:-1] + (-1, 32))
    amax = np.abs(blocks).max(-1, keepdims=True)
    byte = np.maximum(np.where(amax > 0, np.frexp(amax)[1] - 1 + 127, 0) - down, 1)
    scale = np.exp2(byte - 127.0)
    codes = (blocks / scale).astype(np.float32).astype(dtype).astype(np.float64)
    return np.moveaxis((codes * scale).reshape(v.shape), -1, axis)


WIDE = False


def mx_kscale(k):
    if not WIDE:
        return np.ones(k)
    levels = np.array([10, -10, 5, -5, 0])
    if k % 512:
        return np.exp2(np.random.permutation(np.resize(levels, k // 32))).repeat(32)
    a = np.empty((k // 512, 16))
    for p in range(k // 512):
        a[p, :8] = np.random.permutation(np.resize(levels, 8))
        for g in range(8):
            far = levels[np.abs(levels - a[p, g]) >= 10]
            a[p, g + 8] = far[np.random.randint(len(far))]
    return np.exp2(a.ravel()).repeat(32)


def f64(x):
    return np.asarray(x).astype(np.float64)


def striped8(idx):
    return np.concatenate([x.reshape(-1, 16).T for x in idx]).astype(np.uint16)


def runs(offs, k):
    lists = np.stack([offs[16 * r : 16 * r + 16].T.reshape(-1) for r in range(8)]).astype(np.int64)
    return lists[np.arange(k) % 512 // 64]


def pack_weight(w):
    k, n = w.shape
    w = f64(np.asarray(w, np.float32).astype(ml_dtypes.bfloat16)).reshape(k // 32, 32, n)
    amax = np.abs(w).max(1)
    byte = np.clip(np.where(amax > 0, np.frexp(amax)[1] - 1 + 127 - 7, 1), 1, 254)
    scaled = (w * np.exp2(127.0 - byte)[:, None, :]).reshape(k, n).astype(np.float32)
    words = np.ascontiguousarray(scaled.reshape(k // 512, 128, 4, n).transpose(0, 1, 3, 2)).astype(ml_dtypes.float8_e4m3fn).view(np.uint8)
    return words, np.ascontiguousarray(byte.astype(np.uint8).reshape(k // 512, 16, n))


def unpack_weight(words, scales):
    g, p, n, _ = words.shape
    vals = np.ascontiguousarray(words).view(ml_dtypes.float8_e4m3fn).astype(np.float64) * np.repeat(np.exp2(scales.astype(np.float64) - 127.0), 8, axis=1)[..., None]
    return vals.transpose(0, 1, 3, 2).reshape(g * 512, n)


def sigmoid(v):
    return 1.0 / (1.0 + np.exp(-np.maximum(v, -700.0)))

def planes(y):
    n, m = y.shape
    v = y.astype(np.float32).astype(ml_dtypes.bfloat16).astype(np.float64).reshape(n // 32, 32, m)
    top = np.abs(v).max(1)
    byte = np.clip(np.where(top > 0, np.frexp(top)[1] - 1 + 127 - 7, 1), 1, 254)
    codes = (v * np.exp2(127.0 - byte)[:, None, :]).reshape(n, m).astype(np.float32).astype(ml_dtypes.float8_e4m3fn).view(np.uint8)
    words = codes.reshape(n // 512, 128, 4, m).transpose(0, 1, 3, 2)
    return np.ascontiguousarray(words), np.ascontiguousarray(byte.astype(np.uint8).reshape(n // 512, 16, m))


K, T, S, N, H, U = 512, 2048, 512, 512, 512, 1024


def setup_inputs():
    n = np.random.standard_normal
    s = mx_kscale(K)[:, None]
    u = mx_kscale(H)
    packed_xT = pack_weight(n((K, T)) * s)
    packed_w1 = pack_weight(n((K, H)) / np.sqrt(K) / s)
    packed_w2 = pack_weight(n((H, N)) / np.sqrt(H) / u[:, None])
    return {
        "x_words": packed_xT[0],
        "x_scales": packed_xT[1],
        "w1_words": packed_w1[0],
        "w1_scales": packed_w1[1],
        "gn": (np.random.uniform(0.5, 1.5, (H, 1)) * u[:, None]).astype(np.float32),
        "w2_words": packed_w2[0],
        "w2_scales": packed_w2[1],
        "mem": n((N, U)).astype(np.float32),
        "offs": striped8(np.random.randint(0, T, (8, S))),
        "n1": striped8(np.stack([np.random.permutation(S) for _ in range(8)])),
        "n2": striped8(np.stack([np.random.permutation(S) for _ in range(8)])),
        "n3": striped8(np.stack([np.random.permutation(U)[:S] for _ in range(8)])),
    }


def reference(x_words, x_scales, w1_words, w1_scales, gn, w2_words, w2_scales, mem, offs, n1, n2, n3):
    old = f64(mem)[np.arange(N)[:, None], runs(n3, N)]
    xq = unpack_weight(x_words, x_scales)[np.arange(K)[:, None], runs(offs, K)]
    y = unpack_weight(w1_words, w1_scales).T @ xq
    z = f64(gn) * (y - (np.minimum(y[np.arange(H)[:, None], runs(n1, H)], y[np.arange(H)[:, None], runs(n2, H)])))
    h = unpack_weight(w2_words, w2_scales).T @ mxq(z, 0, "e4m3")
    nw = old + sigmoid(h) * (h - old)
    out = f64(mem).copy()
    out[np.arange(N)[:, None], runs(n3, N)] = nw
    return (out,) + planes(out)

@@ -1,0 +1,218 @@
+from contextlib import ExitStack
+
+import concourse.mybir as mybir
+
+K, T, S, N, H, U = 512, 2048, 512, 512, 512, 1024
+FLOPS = 2 * K * H * S + 2 * H * N * S
+
+F32 = mybir.dt.float32
+BF16 = mybir.dt.bfloat16
+I32 = mybir.dt.int32
+U32 = mybir.dt.uint32
+U16 = mybir.dt.uint16
+U8 = mybir.dt.uint8
+FP8X4 = mybir.dt.float8_e4m3fn_x4
+ACT = mybir.ActivationFunctionType
+ALU = mybir.AluOpType
+
+P = 128
+PACK = 4
+HALF = S // 2
+LIST_COLS = S // 16
+QUARTER = U // 4
+
+
+def tile_picked_hashunderpaget_none_po_kernel(
+    tc, x_words, x_scales, w1_words, w1_scales, gn, w2_words, w2_scales, mem, offs, n1, n2, n3, out_0, out_1, out_2
+):
+    nc = tc.nc
+    with ExitStack() as ctx:
+        lists = ctx.enter_context(tc.tile_pool(name="lists", bufs=1))
+        keep = ctx.enter_context(tc.tile_pool(name="keep", bufs=1))
+        ring = ctx.enter_context(tc.tile_pool(name="ring", bufs=3))
+        psum = ctx.enter_context(tc.psum_pool(name="psum", bufs=1))
+
+        def words_view(words):
+            return words[0].rearrange("p c r -> p (c r)").bitcast(I32)
+
+        def load_list(src, name):
+            tile = lists.tile([P, LIST_COLS], U16, name=name)
+            nc.sync.dma_start(tile[:], src)
+            return tile
+
+        def half_of(list_tile, c):
+            return list_tile[:, c * LIST_COLS // 2 : (c + 1) * LIST_COLS // 2]
+
+        def load_weight_scales(scales, name, clearing_engine):
+            raw = keep.tile([P, H], U8, name=name, align_bytes=64)
+            clearing_engine.memset(raw[:].bitcast(I32), 0)
+            rows = scales[0].rearrange("(q r) c -> r q c", r=PACK)
+            for r in range(PACK):
+                nc.gpsimd.dma_start(raw[r:P:32, :].bitcast(I32), rows[r].bitcast(I32))
+            return raw
+
+        def deal(raw, dtype, name):
+            dealt = keep.tile([P, PACK, P], dtype, name=name, align_bytes=64)
+            nc.vector.tensor_copy(
+                out=dealt[:].rearrange("p t m -> p m t"), in_=raw[:].rearrange("p (m t) -> p m t", t=PACK)
+            )
+            return dealt
+
+        offs_t = load_list(offs, "offs_t")
+        xs_all = keep.tile([P, T], U8, align_bytes=64)
+        nc.vector.memset(xs_all[:].bitcast(I32), 0)
+        nc.scalar.dma_start(xs_all[0:P:8, :].bitcast(I32), x_scales[0].bitcast(I32))
+        n1_t = load_list(n1, "n1_t")
+        w1_raw = keep.tile([P, H], I32, align_bytes=64)
+        nc.sync.dma_start(w1_raw[:], words_view(w1_words))
+        xw_all = keep.tile([P, T], I32, align_bytes=64, tag="slot1")
+        nc.sync.dma_start(xw_all[:], words_view(x_words))
+        w2_raw = keep.tile([P, N], I32, align_bytes=64, tag="slot3")
+        nc.sync.dma_start(w2_raw[:], words_view(w2_words))
+        n2_t = load_list(n2, "n2_t")
+        n3_t = load_list(n3, "n3_t")
+        w1s_raw = load_weight_scales(w1_scales, "w1s_raw", nc.gpsimd)
+        gain = keep.tile([P, PACK], F32)
+        nc.gpsimd.dma_start(gain[:], gn.rearrange("(p t) o -> p (t o)", t=PACK))
+
+        warm = keep.tile([P, 1], F32)
+        nc.vector.memset(warm[:], 0.0)
+        warm_out = keep.tile([P, 1], F32)
+        nc.scalar.activation(warm_out[:], warm[:], ACT.Silu)
+
+        xs_picked = keep.tile([P, S], U8, align_bytes=64, tag="slot0")
+        nc.vector.tensor_copy(out=xs_picked[:], in_=xs_all[:].indirect(offs_t[:]))
+        xs_plane = keep.tile([P, S], U8, align_bytes=64)
+        nc.vector.tensor_copy(out=xs_plane[:].bitcast(I32), in_=xs_picked[:].bitcast(I32))
+        for r in range(1, PACK):
+            nc.scalar.dma_start(xs_plane[r:P:32, :].bitcast(I32), xs_picked[8 * r : P : 32, :].bitcast(I32))
+        w1_dealt = deal(w1_raw, I32, "w1_dealt")
+        w1s_dealt = deal(w1s_raw, U8, "w1s_dealt")
+        xw_picked = keep.tile([P, S], U32, align_bytes=64, tag="slot2")
+        nc.vector.tensor_copy(out=xw_picked[:], in_=xw_all[:].bitcast(U32).indirect(offs_t[:]))
+
+        w2s_raw = load_weight_scales(w2_scales, "w2s_raw", nc.vector)
+        neg_gain = keep.tile([P, PACK], F32)
+        nc.scalar.activation(neg_gain[:], gain[:], ACT.Copy, scale=-1.0)
+
+        y_window, y_plain = [], []
+        for t in range(PACK):
+            y_bank = psum.tile([P, S], F32, name="y_bank%d" % t, tag="bank%d" % t)
+            nc.tensor.matmul_mx(
+                out=y_bank[:],
+                lhsT=w1_dealt[:, t, :].bitcast(FP8X4),
+                lhsT_scale=w1s_dealt[:, t, :],
+                rhs=xw_picked[:].bitcast(FP8X4),
+                rhs_scale=xs_plane[:],
+                start=True,
+                stop=True,
+            )
+            y_window.append(keep.tile([P, S], F32, name="y_window%d" % t))
+            y_plain.append(keep.tile([P, S], F32, name="y_plain%d" % t))
+            nc.scalar.copy(y_window[t][:], y_bank[:])
+            nc.scalar.copy(y_plain[t][:], y_bank[:])
+        w2_dealt = deal(w2_raw, I32, "w2_dealt")
+        w2s_dealt = deal(w2s_raw, U8, "w2s_dealt")
+
+        mem_rows = mem.rearrange("(p t) u -> t p u", t=PACK)
+        page = []
+        for t in range(PACK):
+            page.append(keep.tile([P, U], F32, name="page%d" % t, align_bytes=64, tag="slot%d" % t))
+            nc.sync.dma_start(page[t][:], mem_rows[t])
+
+        z_rounded = [keep.tile([P, HALF, PACK], BF16, name="z_rounded%d" % c, align_bytes=64) for c in range(2)]
+        keep_share = [keep.tile([P, S], F32, name="keep_share%d" % t) for t in range(PACK)]
+        new_share = [keep.tile([P, S], F32, name="new_share%d" % t) for t in range(PACK)]
+
+        def make_z(c, t):
+            cols = slice(c * HALF, (c + 1) * HALF)
+            d1 = ring.tile([P, HALF], F32, name="d1")
+            d2 = ring.tile([P, HALF], F32, name="d2")
+            low = ring.tile([P, HALF], F32, name="low", bufs=8)
+            nc.vector.tensor_tensor(d1[:], y_window[t][:].indirect(half_of(n1_t, c)), y_plain[t][:, cols], ALU.subtract)
+            nc.vector.tensor_tensor(d2[:], y_window[t][:].indirect(half_of(n2_t, c)), y_plain[t][:, cols], ALU.subtract)
+            nc.vector.tensor_tensor(low[:], d1[:], d2[:], ALU.min)
+            nc.scalar.activation(z_rounded[c][:, :, t], low[:], ACT.Copy, scale=neg_gain[:, t : t + 1])
+
+        def second_product(c):
+            cols = slice(c * HALF, (c + 1) * HALF)
+            z_words = keep.tile([P, HALF], U32, name="z_words%d" % c, align_bytes=64)
+            z_scales = keep.tile([P, HALF], U8, name="z_scales%d" % c, align_bytes=64)
+            nc.vector.quantize_mx(
+                out=z_words[:].bitcast(FP8X4), scales=z_scales[:], in_=z_rounded[c][:].rearrange("p j t -> p (j t)")
+            )
+            for t in range(PACK):
+                h_bank = psum.tile([P, HALF], F32, name="h_bank%d_%d" % (c, t), tag="bank%d" % (PACK * (1 - c) + t))
+                nc.tensor.matmul_mx(
+                    out=h_bank[:],
+                    lhsT=w2_dealt[:, t, :].bitcast(FP8X4),
+                    lhsT_scale=w2s_dealt[:, t, :],
+                    rhs=z_words[:].bitcast(FP8X4),
+                    rhs_scale=z_scales[:],
+                    start=True,
+                    stop=True,
+                )
+                tanh_half = ring.tile([P, HALF], F32, name="tanh_half")
+                nc.scalar.activation(tanh_half[:], h_bank[:], ACT.Tanh, scale=0.5)
+                nc.scalar.activation(keep_share[t][:, cols], tanh_half[:], ACT.Copy, scale=-0.5, bias=0.5)
+                nc.scalar.activation(new_share[t][:, cols], h_bank[:], ACT.Silu)
+
+        kept = [keep.tile([P, S], F32, name="kept%d" % t) for t in range(PACK)]
+
+        def fetch_old(t, entries, cols):
+            nc.vector.tensor_tensor(kept[t][:, cols], page[t][:].indirect(entries), keep_share[t][:, cols], ALU.mult)
+
+        def put_new(t, entries, cols):
+            nc.vector.tensor_tensor(page[t][:].indirect(entries), kept[t][:, cols], new_share[t][:, cols], ALU.add)
+
+        out_rows = out_0.rearrange("(p t) u -> t p u", t=PACK)
+        out_rounded = [keep.tile([P, QUARTER, PACK], BF16, name="out_rounded%d" % q, align_bytes=64) for q in range(4)]
+
+        def finish_tile(t):
+            nc.sync.dma_start(out_rows[t], page[t][:])
+            for q in range(4):
+                src = page[t][:, q * QUARTER : (q + 1) * QUARTER]
+                if t == PACK - 1 and q < 2:
+                    nc.vector.tensor_copy(out=out_rounded[q][:, :, t], in_=src)
+                elif t == PACK - 2 and q < 2:
+                    nc.scalar.copy(out_rounded[q][:, :, t : t + 2], src.unsqueeze(2).to_broadcast([P, QUARTER, 2]))
+                else:
+                    nc.scalar.copy(out_rounded[q][:, :, t], src)
+
+        first, second, both = slice(0, HALF), slice(HALF, S), slice(0, S)
+        for t in range(PACK):
+            make_z(0, t)
+        make_z(1, 0)
+        second_product(0)
+        for t in range(1, PACK):
+            make_z(1, t)
+        for t in range(2):
+            fetch_old(t, half_of(n3_t, 0), first)
+        second_product(1)
+        for t in range(2):
+            put_new(t, half_of(n3_t, 0), first)
+        for t in range(2):
+            fetch_old(t, half_of(n3_t, 1), second)
+            put_new(t, half_of(n3_t, 1), second)
+            finish_tile(t)
+        for t in range(2, PACK):
+            fetch_old(t, n3_t[:], both)
+        for t in range(2, PACK):
+            put_new(t, n3_t[:], both)
+            finish_tile(t)
+
+        out_scales = keep.tile([P, U], U8, align_bytes=64)
+        out_words_dram = words_view(out_1)
+        for q in (0, 2, 1, 3):
+            cols = slice(q * QUARTER, (q + 1) * QUARTER)
+            out_words = keep.tile([P, QUARTER], I32, name="out_words%d" % q, align_bytes=64)
+            nc.vector.quantize_mx(
+                out=out_words[:].bitcast(FP8X4),
+                scales=out_scales[:, cols],
+                in_=out_rounded[q][:].rearrange("p c t -> p (c t)"),
+            )
+            nc.sync.dma_start(out_words_dram[:, cols], out_words[:])
+        scale_rows = out_2[0].rearrange("(q r) c -> r q c", r=PACK)
+        for r in range(PACK):
+            engine = nc.scalar if r % 2 else nc.sync
+            engine.dma_start(scale_rows[r].bitcast(I32), out_scales[r:P:32, :].bitcast(I32))

@@ -40,40 +40,40 @@ def tile_picked_hashunderpaget_none_po_kernel(
             nc.sync.dma_start(tile[:], src)
             return tile
 
-        def half_of(list_tile, c):
+        def entries_of(list_tile, c):
             return list_tile[:, c * LIST_COLS // 2 : (c + 1) * LIST_COLS // 2]
 
-        def load_weight_scales(scales, name, clearing_engine):
-            raw = keep.tile([P, H], U8, name=name, align_bytes=64)
-            clearing_engine.memset(raw[:].bitcast(I32), 0)
+        def cols_of(c):
+            return slice(c * HALF, (c + 1) * HALF)
+
+        def load_weight_scales(scales, name, queues):
+            raw = keep.tile([P, H], U8, name=name, align_bytes=64, tag=name)
+            nc.vector.memset(raw[:].bitcast(I32), 0)
             rows = scales[0].rearrange("(q r) c -> r q c", r=PACK)
             for r in range(PACK):
-                nc.gpsimd.dma_start(raw[r:P:32, :].bitcast(I32), rows[r].bitcast(I32))
+                queues[r].dma_start(raw[r:P:32, :].bitcast(I32), rows[r].bitcast(I32))
             return raw
 
-        def deal(raw, dtype, name):
-            dealt = keep.tile([P, PACK, P], dtype, name=name, align_bytes=64)
+        def deal(raw, dtype, name, tag):
+            dealt = keep.tile([P, PACK, P], dtype, name=name, align_bytes=64, tag=tag)
             nc.vector.tensor_copy(
                 out=dealt[:].rearrange("p t m -> p m t"), in_=raw[:].rearrange("p (m t) -> p m t", t=PACK)
             )
             return dealt
 
         offs_t = load_list(offs, "offs_t")
-        xs_all = keep.tile([P, T], U8, align_bytes=64)
-        nc.vector.memset(xs_all[:].bitcast(I32), 0)
-        nc.scalar.dma_start(xs_all[0:P:8, :].bitcast(I32), x_scales[0].bitcast(I32))
         n1_t = load_list(n1, "n1_t")
-        w1_raw = keep.tile([P, H], I32, align_bytes=64)
-        nc.sync.dma_start(w1_raw[:], words_view(w1_words))
-        xw_all = keep.tile([P, T], I32, align_bytes=64, tag="slot1")
-        nc.sync.dma_start(xw_all[:], words_view(x_words))
-        w2_raw = keep.tile([P, N], I32, align_bytes=64, tag="slot3")
-        nc.sync.dma_start(w2_raw[:], words_view(w2_words))
         n2_t = load_list(n2, "n2_t")
         n3_t = load_list(n3, "n3_t")
-        w1s_raw = load_weight_scales(w1_scales, "w1s_raw", nc.gpsimd)
-        gain = keep.tile([P, PACK], F32)
-        nc.gpsimd.dma_start(gain[:], gn.rearrange("(p t) o -> p (t o)", t=PACK))
+        xs_all = keep.tile([P, T], U8, align_bytes=64, tag="xs_all")
+        nc.gpsimd.memset(xs_all[:].bitcast(I32), 0)
+        nc.scalar.dma_start(xs_all[0:P:8, :].bitcast(I32), x_scales[0].bitcast(I32))
+        w1_raw = keep.tile([P, H], I32, align_bytes=64)
+        nc.sync.dma_start(w1_raw[:], words_view(w1_words))
+        xw_all = keep.tile([P, T], I32, align_bytes=64, tag="xw_all")
+        nc.sync.dma_start(xw_all[:], words_view(x_words))
+        w1s_raw = load_weight_scales(w1_scales, "w1s_raw", (nc.gpsimd, nc.gpsimd, nc.scalar, nc.scalar))
+        w2s_raw = load_weight_scales(w2_scales, "w2s_raw", (nc.gpsimd,) * PACK)
 
         warm = keep.tile([P, 1], F32)
         nc.vector.memset(warm[:], 0.0)
@@ -86,33 +86,34 @@ def tile_picked_hashunderpaget_none_po_kernel(
         nc.vector.tensor_copy(out=xs_plane[:].bitcast(I32), in_=xs_picked[:].bitcast(I32))
         for r in range(1, PACK):
             nc.scalar.dma_start(xs_plane[r:P:32, :].bitcast(I32), xs_picked[8 * r : P : 32, :].bitcast(I32))
-        w1_dealt = deal(w1_raw, I32, "w1_dealt")
-        w1s_dealt = deal(w1s_raw, U8, "w1s_dealt")
-        xw_picked = keep.tile([P, S], U32, align_bytes=64, tag="slot2")
-        nc.vector.tensor_copy(out=xw_picked[:], in_=xw_all[:].bitcast(U32).indirect(offs_t[:]))
+        w2_raw = keep.tile([P, N], I32, align_bytes=64, tag="xs_all")
+        nc.sync.dma_start(w2_raw[:], words_view(w2_words))
+        w1_dealt = deal(w1_raw, I32, "w1_dealt", "slot1")
+        w1s_dealt = deal(w1s_raw, U8, "w1s_dealt", "w1s_dealt")
+        gain = keep.tile([P, PACK], F32, align_bytes=64, tag="w1s_raw")
+        nc.sync.dma_start(gain[:], gn.rearrange("(p t) o -> p (t o)", t=PACK))
+        xw_picked = []
+        for c in range(2):
+            xw_picked.append(keep.tile([P, HALF], U32, name="xw_picked%d" % c, align_bytes=64, tag="slot%d" % (2 + c)))
+            nc.vector.tensor_copy(out=xw_picked[c][:], in_=xw_all[:].bitcast(U32).indirect(entries_of(offs_t, c)))
 
-        w2s_raw = load_weight_scales(w2_scales, "w2s_raw", nc.vector)
+        y_bank = {}
+        for pair in range(0, PACK, 2):
+            for c in range(2):
+                for t in range(pair, pair + 2):
+                    y_bank[c, t] = psum.tile([P, HALF], F32, name="y_bank%d_%d" % (c, t), tag="bank%d" % (PACK * c + t))
+                    nc.tensor.matmul_mx(
+                        out=y_bank[c, t][:],
+                        lhsT=w1_dealt[:, t, :].bitcast(FP8X4),
+                        lhsT_scale=w1s_dealt[:, t, :],
+                        rhs=xw_picked[c][:].bitcast(FP8X4),
+                        rhs_scale=xs_plane[:, cols_of(c)],
+                        start=True,
+                        stop=True,
+                    )
+        w2_dealt = deal(w2_raw, I32, "w2_dealt", "xw_all")
         neg_gain = keep.tile([P, PACK], F32)
         nc.scalar.activation(neg_gain[:], gain[:], ACT.Copy, scale=-1.0)
-
-        y_window, y_plain = [], []
-        for t in range(PACK):
-            y_bank = psum.tile([P, S], F32, name="y_bank%d" % t, tag="bank%d" % t)
-            nc.tensor.matmul_mx(
-                out=y_bank[:],
-                lhsT=w1_dealt[:, t, :].bitcast(FP8X4),
-                lhsT_scale=w1s_dealt[:, t, :],
-                rhs=xw_picked[:].bitcast(FP8X4),
-                rhs_scale=xs_plane[:],
-                start=True,
-                stop=True,
-            )
-            y_window.append(keep.tile([P, S], F32, name="y_window%d" % t))
-            y_plain.append(keep.tile([P, S], F32, name="y_plain%d" % t))
-            nc.scalar.copy(y_window[t][:], y_bank[:])
-            nc.scalar.copy(y_plain[t][:], y_bank[:])
-        w2_dealt = deal(w2_raw, I32, "w2_dealt")
-        w2s_dealt = deal(w2s_raw, U8, "w2s_dealt")
 
         mem_rows = mem.rearrange("(p t) u -> t p u", t=PACK)
         page = []
@@ -120,31 +121,40 @@ def tile_picked_hashunderpaget_none_po_kernel(
             page.append(keep.tile([P, U], F32, name="page%d" % t, align_bytes=64, tag="slot%d" % t))
             nc.sync.dma_start(page[t][:], mem_rows[t])
 
+        y_window = [keep.tile([P, S], F32, name="y_window%d" % t) for t in range(PACK)]
         z_rounded = [keep.tile([P, HALF, PACK], BF16, name="z_rounded%d" % c, align_bytes=64) for c in range(2)]
-        keep_share = [keep.tile([P, S], F32, name="keep_share%d" % t) for t in range(PACK)]
-        new_share = [keep.tile([P, S], F32, name="new_share%d" % t) for t in range(PACK)]
+        y_plain, diffs, low, h_bank = {}, {}, {}, {}
 
-        def make_z(c, t):
-            cols = slice(c * HALF, (c + 1) * HALF)
-            d1 = ring.tile([P, HALF], F32, name="d1")
-            d2 = ring.tile([P, HALF], F32, name="d2")
-            low = ring.tile([P, HALF], F32, name="low", bufs=8)
-            nc.vector.tensor_tensor(d1[:], y_window[t][:].indirect(half_of(n1_t, c)), y_plain[t][:, cols], ALU.subtract)
-            nc.vector.tensor_tensor(d2[:], y_window[t][:].indirect(half_of(n2_t, c)), y_plain[t][:, cols], ALU.subtract)
-            nc.vector.tensor_tensor(low[:], d1[:], d2[:], ALU.min)
-            nc.scalar.activation(z_rounded[c][:, :, t], low[:], ACT.Copy, scale=neg_gain[:, t : t + 1])
+        def copy_window(t):
+            for c in range(2):
+                nc.scalar.copy(y_window[t][:, cols_of(c)], y_bank[c, t][:])
+
+        def copy_plain(c, t, tag):
+            y_plain[c, t] = keep.tile([P, HALF], F32, name="y_plain%d_%d" % (c, t), align_bytes=64, tag=tag)
+            nc.scalar.copy(y_plain[c, t][:], y_bank[c, t][:])
+
+        def fetch_diff(c, t, which):
+            diffs[c, t, which] = ring.tile([P, HALF], F32, name="diff%d" % which)
+            entries = entries_of((n1_t, n2_t)[which], c)
+            nc.vector.tensor_tensor(diffs[c, t, which][:], y_window[t][:].indirect(entries), y_plain[c, t][:], ALU.subtract)
+
+        def take_low(c, t):
+            low[c, t] = keep.tile([P, HALF], F32, name="low%d_%d" % (c, t), align_bytes=64, tag="low%d_%d" % (c, t))
+            nc.vector.tensor_tensor(low[c, t][:], diffs[c, t, 0][:], diffs[c, t, 1][:], ALU.min)
+
+        def round_z(c, t):
+            nc.scalar.activation(z_rounded[c][:, :, t], low[c, t][:], ACT.Copy, scale=neg_gain[:, t : t + 1])
 
         def second_product(c):
-            cols = slice(c * HALF, (c + 1) * HALF)
             z_words = keep.tile([P, HALF], U32, name="z_words%d" % c, align_bytes=64)
             z_scales = keep.tile([P, HALF], U8, name="z_scales%d" % c, align_bytes=64)
             nc.vector.quantize_mx(
                 out=z_words[:].bitcast(FP8X4), scales=z_scales[:], in_=z_rounded[c][:].rearrange("p j t -> p (j t)")
             )
             for t in range(PACK):
-                h_bank = psum.tile([P, HALF], F32, name="h_bank%d_%d" % (c, t), tag="bank%d" % (PACK * (1 - c) + t))
+                h_bank[c, t] = psum.tile([P, HALF], F32, name="h_bank%d_%d" % (c, t), tag="bank%d" % (PACK * c + t))
                 nc.tensor.matmul_mx(
-                    out=h_bank[:],
+                    out=h_bank[c, t][:],
                     lhsT=w2_dealt[:, t, :].bitcast(FP8X4),
                     lhsT_scale=w2s_dealt[:, t, :],
                     rhs=z_words[:].bitcast(FP8X4),
@@ -152,18 +162,23 @@ def tile_picked_hashunderpaget_none_po_kernel(
                     start=True,
                     stop=True,
                 )
-                tanh_half = ring.tile([P, HALF], F32, name="tanh_half")
-                nc.scalar.activation(tanh_half[:], h_bank[:], ACT.Tanh, scale=0.5)
-                nc.scalar.activation(keep_share[t][:, cols], tanh_half[:], ACT.Copy, scale=-0.5, bias=0.5)
-                nc.scalar.activation(new_share[t][:, cols], h_bank[:], ACT.Silu)
 
-        kept = [keep.tile([P, S], F32, name="kept%d" % t) for t in range(PACK)]
+        old_factor = [keep.tile([P, S], F32, name="old_factor%d" % t) for t in range(PACK)]
+        old_part = [keep.tile([P, S], F32, name="old_part%d" % t) for t in range(PACK)]
+
+        def make_old_factor(c, t):
+            tanh_half = ring.tile([P, HALF], F32, name="tanh_half")
+            nc.scalar.activation(tanh_half[:], h_bank[c, t][:], ACT.Tanh, scale=0.5)
+            nc.scalar.activation(old_factor[t][:, cols_of(c)], tanh_half[:], ACT.Copy, scale=-0.5, bias=0.5)
+
+        def make_new_part(c, t, dest):
+            nc.scalar.activation(dest, h_bank[c, t][:], ACT.Silu)
 
         def fetch_old(t, entries, cols):
-            nc.vector.tensor_tensor(kept[t][:, cols], page[t][:].indirect(entries), keep_share[t][:, cols], ALU.mult)
+            nc.vector.tensor_tensor(old_part[t][:, cols], page[t][:].indirect(entries), old_factor[t][:, cols], ALU.mult)
 
-        def put_new(t, entries, cols):
-            nc.vector.tensor_tensor(page[t][:].indirect(entries), kept[t][:, cols], new_share[t][:, cols], ALU.add)
+        def put_new(t, entries, cols, new_part):
+            nc.vector.tensor_tensor(page[t][:].indirect(entries), old_part[t][:, cols], new_part, ALU.add)
 
         out_rows = out_0.rearrange("(p t) u -> t p u", t=PACK)
         out_rounded = [keep.tile([P, QUARTER, PACK], BF16, name="out_rounded%d" % q, align_bytes=64) for q in range(4)]
@@ -179,39 +194,88 @@ def tile_picked_hashunderpaget_none_po_kernel(
                 else:
                     nc.scalar.copy(out_rounded[q][:, :, t], src)
 
-        first, second, both = slice(0, HALF), slice(HALF, S), slice(0, S)
         for t in range(PACK):
-            make_z(0, t)
-        make_z(1, 0)
-        second_product(0)
+            copy_window(t)
+            copy_plain(0, t, "y_plain0_%d" % t)
+        copy_plain(1, 0, "y_plain1_0")
+
+        fetch_diff(0, 0, 0)
+        fetch_diff(0, 0, 1)
         for t in range(1, PACK):
-            make_z(1, t)
+            fetch_diff(0, t, 0)
+            take_low(0, t - 1)
+            round_z(0, t - 1)
+            fetch_diff(0, t, 1)
+        w2s_dealt = deal(w2s_raw, U8, "w2s_dealt", "low0_1")
+        fetch_diff(1, 0, 0)
+        take_low(0, PACK - 1)
+        round_z(0, PACK - 1)
+        fetch_diff(1, 0, 1)
+        copy_plain(1, 1, "low0_3")
+        copy_plain(1, 2, "y_plain1_2")
+        copy_plain(1, 3, "y_plain1_3")
+        take_low(1, 0)
+        second_product(0)
+        round_z(1, 0)
+        fetch_diff(1, 1, 0)
+        fetch_diff(1, 1, 1)
+        make_old_factor(0, 0)
+        for t in range(2, PACK):
+            fetch_diff(1, t, 0)
+            take_low(1, t - 1)
+            round_z(1, t - 1)
+            fetch_diff(1, t, 1)
+            if t == 2:
+                make_old_factor(0, 1)
+        fetch_old(0, entries_of(n3_t, 0), cols_of(0))
+        take_low(1, PACK - 1)
+        round_z(1, PACK - 1)
+        fetch_old(1, entries_of(n3_t, 0), cols_of(0))
+        new_first = [
+            keep.tile([P, HALF], F32, name="new_first0", align_bytes=64, tag="low1_3"),
+            keep.tile([P, HALF], F32, name="new_first1"),
+        ]
+        new_rest = [keep.tile([P, S], F32, name="new_rest%d" % t) for t in range(PACK)]
         for t in range(2):
-            fetch_old(t, half_of(n3_t, 0), first)
+            make_new_part(0, t, new_first[t][:])
+        for t in range(2, PACK):
+            make_old_factor(0, t)
+            make_new_part(0, t, new_rest[t][:, cols_of(0)])
         second_product(1)
         for t in range(2):
-            put_new(t, half_of(n3_t, 0), first)
-        for t in range(2):
-            fetch_old(t, half_of(n3_t, 1), second)
-            put_new(t, half_of(n3_t, 1), second)
-            finish_tile(t)
+            put_new(t, entries_of(n3_t, 0), cols_of(0), new_first[t][:])
+        make_old_factor(1, 0)
+        make_old_factor(1, 1)
+        make_new_part(1, 0, new_rest[0][:, cols_of(1)])
+        make_old_factor(1, 2)
+        make_new_part(1, 1, new_rest[1][:, cols_of(1)])
+        make_old_factor(1, 3)
+        make_new_part(1, 2, new_rest[2][:, cols_of(1)])
+        make_new_part(1, 3, new_rest[3][:, cols_of(1)])
+        fetch_old(0, entries_of(n3_t, 1), cols_of(1))
+        fetch_old(1, entries_of(n3_t, 1), cols_of(1))
+        put_new(0, entries_of(n3_t, 1), cols_of(1), new_rest[0][:, cols_of(1)])
+        finish_tile(0)
+        fetch_old(2, n3_t[:], slice(0, S))
+        put_new(1, entries_of(n3_t, 1), cols_of(1), new_rest[1][:, cols_of(1)])
+        finish_tile(1)
+        fetch_old(3, n3_t[:], slice(0, S))
         for t in range(2, PACK):
-            fetch_old(t, n3_t[:], both)
-        for t in range(2, PACK):
-            put_new(t, n3_t[:], both)
+            put_new(t, n3_t[:], slice(0, S), new_rest[t][:])
             finish_tile(t)
 
         out_scales = keep.tile([P, U], U8, align_bytes=64)
         out_words_dram = words_view(out_1)
-        for q in (0, 2, 1, 3):
-            cols = slice(q * QUARTER, (q + 1) * QUARTER)
-            out_words = keep.tile([P, QUARTER], I32, name="out_words%d" % q, align_bytes=64)
-            nc.vector.quantize_mx(
-                out=out_words[:].bitcast(FP8X4),
-                scales=out_scales[:, cols],
-                in_=out_rounded[q][:].rearrange("p c t -> p (c t)"),
-            )
-            nc.sync.dma_start(out_words_dram[:, cols], out_words[:])
+        for half in range(2):
+            out_words = keep.tile([P, 2 * QUARTER], I32, name="out_words%d" % half, align_bytes=64)
+            for i in range(2):
+                q = 2 * half + i
+                nc.vector.quantize_mx(
+                    out=out_words[:, i * QUARTER : (i + 1) * QUARTER].bitcast(FP8X4),
+                    scales=out_scales[:, q * QUARTER : (q + 1) * QUARTER],
+                    in_=out_rounded[q][:].rearrange("p c t -> p (c t)"),
+                )
+            nc.sync.dma_start(out_words_dram[:, 2 * half * QUARTER : 2 * (half + 1) * QUARTER], out_words[:])
         scale_rows = out_2[0].rearrange("(q r) c -> r q c", r=PACK)
         for r in range(PACK):
             engine = nc.scalar if r % 2 else nc.sync

@@ -19,7 +19,7 @@ P = 128
 PACK = 4
 HALF = S // 2
 LIST_COLS = S // 16
-QUARTER = U // 4
+PIECES = (slice(0, U // 2), slice(U // 2, 3 * U // 4), slice(3 * U // 4, U))
 
 
 def tile_picked_hashunderpaget_none_po_kernel(
@@ -46,12 +46,11 @@ def tile_picked_hashunderpaget_none_po_kernel(
         def cols_of(c):
             return slice(c * HALF, (c + 1) * HALF)
 
-        def load_weight_scales(scales, name, queues):
-            raw = keep.tile([P, H], U8, name=name, align_bytes=64, tag=name)
-            nc.vector.memset(raw[:].bitcast(I32), 0)
-            rows = scales[0].rearrange("(q r) c -> r q c", r=PACK)
+        def load_weight_scales(scales, name, tag):
+            raw = keep.tile([P, H], U8, name=name, align_bytes=64, tag=tag)
+            rows = scales[0].bitcast(I32).rearrange("(q r) c -> r q c", r=PACK)
             for r in range(PACK):
-                queues[r].dma_start(raw[r:P:32, :].bitcast(I32), rows[r].bitcast(I32))
+                nc.sync.dma_start(raw[r:P:PACK, :].bitcast(I32), rows[r].unsqueeze(1).to_broadcast([4, 8, H // 4]))
             return raw
 
         def deal(raw, dtype, name, tag):
@@ -62,19 +61,21 @@ def tile_picked_hashunderpaget_none_po_kernel(
             return dealt
 
         offs_t = load_list(offs, "offs_t")
-        n1_t = load_list(n1, "n1_t")
-        n2_t = load_list(n2, "n2_t")
-        n3_t = load_list(n3, "n3_t")
-        xs_all = keep.tile([P, T], U8, align_bytes=64, tag="xs_all")
-        nc.gpsimd.memset(xs_all[:].bitcast(I32), 0)
-        nc.scalar.dma_start(xs_all[0:P:8, :].bitcast(I32), x_scales[0].bitcast(I32))
-        w1_raw = keep.tile([P, H], I32, align_bytes=64)
+        xs_all = keep.tile([P, T], U8, align_bytes=64)
+        nc.sync.dma_start(xs_all[:].bitcast(I32), x_scales[0].bitcast(I32).unsqueeze(1).to_broadcast([16, 8, T // 4]))
+        w1s_raw = load_weight_scales(w1_scales, "w1s_raw", "w1s_raw")
+        w1_raw = keep.tile([P, H], I32, align_bytes=64, tag="w1_raw")
         nc.sync.dma_start(w1_raw[:], words_view(w1_words))
         xw_all = keep.tile([P, T], I32, align_bytes=64, tag="xw_all")
         nc.sync.dma_start(xw_all[:], words_view(x_words))
-        w1s_raw = load_weight_scales(w1_scales, "w1s_raw", (nc.gpsimd, nc.gpsimd, nc.scalar, nc.scalar))
-        w2s_raw = load_weight_scales(w2_scales, "w2s_raw", (nc.gpsimd,) * PACK)
+        n1_t = load_list(n1, "n1_t")
+        n2_t = load_list(n2, "n2_t")
+        n3_t = load_list(n3, "n3_t")
+        w2_raw = keep.tile([P, N], I32, align_bytes=64, tag="w2_raw")
+        nc.sync.dma_start(w2_raw[:], words_view(w2_words))
 
+        gain = keep.tile([P, PACK], F32)
+        nc.gpsimd.dma_start(gain[:], gn.rearrange("(p t) o -> p (t o)", t=PACK))
         warm = keep.tile([P, 1], F32)
         nc.vector.memset(warm[:], 0.0)
         warm_out = keep.tile([P, 1], F32)
@@ -86,34 +87,28 @@ def tile_picked_hashunderpaget_none_po_kernel(
         nc.vector.tensor_copy(out=xs_plane[:].bitcast(I32), in_=xs_picked[:].bitcast(I32))
         for r in range(1, PACK):
             nc.scalar.dma_start(xs_plane[r:P:32, :].bitcast(I32), xs_picked[8 * r : P : 32, :].bitcast(I32))
-        w2_raw = keep.tile([P, N], I32, align_bytes=64, tag="xs_all")
-        nc.sync.dma_start(w2_raw[:], words_view(w2_words))
         w1_dealt = deal(w1_raw, I32, "w1_dealt", "slot1")
+        w2s_raw = load_weight_scales(w2_scales, "w2s_raw", "w1_raw")
         w1s_dealt = deal(w1s_raw, U8, "w1s_dealt", "w1s_dealt")
-        gain = keep.tile([P, PACK], F32, align_bytes=64, tag="w1s_raw")
-        nc.sync.dma_start(gain[:], gn.rearrange("(p t) o -> p (t o)", t=PACK))
         xw_picked = []
         for c in range(2):
             xw_picked.append(keep.tile([P, HALF], U32, name="xw_picked%d" % c, align_bytes=64, tag="slot%d" % (2 + c)))
             nc.vector.tensor_copy(out=xw_picked[c][:], in_=xw_all[:].bitcast(U32).indirect(entries_of(offs_t, c)))
 
         y_bank = {}
-        for pair in range(0, PACK, 2):
+        for t in range(PACK):
             for c in range(2):
-                for t in range(pair, pair + 2):
-                    y_bank[c, t] = psum.tile([P, HALF], F32, name="y_bank%d_%d" % (c, t), tag="bank%d" % (PACK * c + t))
-                    nc.tensor.matmul_mx(
-                        out=y_bank[c, t][:],
-                        lhsT=w1_dealt[:, t, :].bitcast(FP8X4),
-                        lhsT_scale=w1s_dealt[:, t, :],
-                        rhs=xw_picked[c][:].bitcast(FP8X4),
-                        rhs_scale=xs_plane[:, cols_of(c)],
-                        start=True,
-                        stop=True,
-                    )
+                y_bank[c, t] = psum.tile([P, HALF], F32, name="y_bank%d_%d" % (c, t), tag="bank%d" % (PACK * c + t))
+                nc.tensor.matmul_mx(
+                    out=y_bank[c, t][:],
+                    lhsT=w1_dealt[:, t, :].bitcast(FP8X4),
+                    lhsT_scale=w1s_dealt[:, t, :],
+                    rhs=xw_picked[c][:].bitcast(FP8X4),
+                    rhs_scale=xs_plane[:, cols_of(c)],
+                    start=True,
+                    stop=True,
+                )
         w2_dealt = deal(w2_raw, I32, "w2_dealt", "xw_all")
-        neg_gain = keep.tile([P, PACK], F32)
-        nc.scalar.activation(neg_gain[:], gain[:], ACT.Copy, scale=-1.0)
 
         mem_rows = mem.rearrange("(p t) u -> t p u", t=PACK)
         page = []
@@ -127,11 +122,14 @@ def tile_picked_hashunderpaget_none_po_kernel(
 
         def copy_window(t):
             for c in range(2):
-                nc.scalar.copy(y_window[t][:, cols_of(c)], y_bank[c, t][:])
+                if (c, t) == (1, 0):
+                    nc.vector.tensor_scalar_mul(y_window[t][:, cols_of(c)], y_bank[c, t][:], -1.0)
+                else:
+                    nc.scalar.activation(y_window[t][:, cols_of(c)], y_bank[c, t][:], ACT.Copy, scale=-1.0)
 
         def copy_plain(c, t, tag):
             y_plain[c, t] = keep.tile([P, HALF], F32, name="y_plain%d_%d" % (c, t), align_bytes=64, tag=tag)
-            nc.scalar.copy(y_plain[c, t][:], y_bank[c, t][:])
+            nc.scalar.activation(y_plain[c, t][:], y_bank[c, t][:], ACT.Copy, scale=-1.0)
 
         def fetch_diff(c, t, which):
             diffs[c, t, which] = ring.tile([P, HALF], F32, name="diff%d" % which)
@@ -140,10 +138,10 @@ def tile_picked_hashunderpaget_none_po_kernel(
 
         def take_low(c, t):
             low[c, t] = keep.tile([P, HALF], F32, name="low%d_%d" % (c, t), align_bytes=64, tag="low%d_%d" % (c, t))
-            nc.vector.tensor_tensor(low[c, t][:], diffs[c, t, 0][:], diffs[c, t, 1][:], ALU.min)
+            nc.vector.tensor_tensor(low[c, t][:], diffs[c, t, 0][:], diffs[c, t, 1][:], ALU.max)
 
         def round_z(c, t):
-            nc.scalar.activation(z_rounded[c][:, :, t], low[c, t][:], ACT.Copy, scale=neg_gain[:, t : t + 1])
+            nc.scalar.activation(z_rounded[c][:, :, t], low[c, t][:], ACT.Copy, scale=gain[:, t : t + 1])
 
         def second_product(c):
             z_words = keep.tile([P, HALF], U32, name="z_words%d" % c, align_bytes=64)
@@ -152,9 +150,15 @@ def tile_picked_hashunderpaget_none_po_kernel(
                 out=z_words[:].bitcast(FP8X4), scales=z_scales[:], in_=z_rounded[c][:].rearrange("p j t -> p (j t)")
             )
             for t in range(PACK):
-                h_bank[c, t] = psum.tile([P, HALF], F32, name="h_bank%d_%d" % (c, t), tag="bank%d" % (PACK * c + t))
+                if t < 2:
+                    h_bank[c, t] = psum.tile([P, HALF], F32, name="h_bank%d_%d" % (c, t), tag="bank%d" % (PACK * c + t))
+                    h_half = h_bank[c, t][:]
+                else:
+                    if c == 0:
+                        h_bank[t] = psum.tile([P, S], F32, name="h_bank%d" % t, tag="bank%d" % t)
+                    h_half = h_bank[t][:, cols_of(c)]
                 nc.tensor.matmul_mx(
-                    out=h_bank[c, t][:],
+                    out=h_half,
                     lhsT=w2_dealt[:, t, :].bitcast(FP8X4),
                     lhsT_scale=w2s_dealt[:, t, :],
                     rhs=z_words[:].bitcast(FP8X4),
@@ -166,33 +170,41 @@ def tile_picked_hashunderpaget_none_po_kernel(
         old_factor = [keep.tile([P, S], F32, name="old_factor%d" % t) for t in range(PACK)]
         old_part = [keep.tile([P, S], F32, name="old_part%d" % t) for t in range(PACK)]
 
-        def make_old_factor(c, t):
-            tanh_half = ring.tile([P, HALF], F32, name="tanh_half")
-            nc.scalar.activation(tanh_half[:], h_bank[c, t][:], ACT.Tanh, scale=0.5)
-            nc.scalar.activation(old_factor[t][:, cols_of(c)], tanh_half[:], ACT.Copy, scale=-0.5, bias=0.5)
+        tanh_half = [keep.tile([P, S], F32, name="tanh_half%d" % t) for t in range(PACK)]
 
-        def make_new_part(c, t, dest):
-            nc.scalar.activation(dest, h_bank[c, t][:], ACT.Silu)
+        new_part = {t: keep.tile([P, S], F32, name="new_part%d" % t) for t in (0, 2, 3)}
+
+        def make_tanh(bank, t, cols):
+            nc.scalar.activation(tanh_half[t][:, cols], bank[:], ACT.Tanh, scale=0.5)
+
+        def make_old_factor(t, cols):
+            nc.scalar.activation(old_factor[t][:, cols], tanh_half[t][:, cols], ACT.Copy, scale=-0.5, bias=0.5)
+
+        def make_new_part(bank, t, cols):
+            nc.scalar.activation(new_part[t][:, cols], bank[:], ACT.Silu)
 
         def fetch_old(t, entries, cols):
             nc.vector.tensor_tensor(old_part[t][:, cols], page[t][:].indirect(entries), old_factor[t][:, cols], ALU.mult)
 
-        def put_new(t, entries, cols, new_part):
-            nc.vector.tensor_tensor(page[t][:].indirect(entries), old_part[t][:, cols], new_part, ALU.add)
+        def put_new(t, entries, cols):
+            nc.vector.tensor_tensor(page[t][:].indirect(entries), old_part[t][:, cols], new_part[t][:, cols], ALU.add)
 
         out_rows = out_0.rearrange("(p t) u -> t p u", t=PACK)
-        out_rounded = [keep.tile([P, QUARTER, PACK], BF16, name="out_rounded%d" % q, align_bytes=64) for q in range(4)]
+        out_rounded = [
+            keep.tile([P, cols.stop - cols.start, PACK], BF16, name="out_rounded%d" % piece, align_bytes=64)
+            for piece, cols in enumerate(PIECES)
+        ]
 
         def finish_tile(t):
             nc.sync.dma_start(out_rows[t], page[t][:])
-            for q in range(4):
-                src = page[t][:, q * QUARTER : (q + 1) * QUARTER]
-                if t == PACK - 1 and q < 2:
-                    nc.vector.tensor_copy(out=out_rounded[q][:, :, t], in_=src)
-                elif t == PACK - 2 and q < 2:
-                    nc.scalar.copy(out_rounded[q][:, :, t : t + 2], src.unsqueeze(2).to_broadcast([P, QUARTER, 2]))
+            for piece, cols in enumerate(PIECES):
+                src = page[t][:, cols]
+                if t == PACK - 1 and piece == 0:
+                    nc.vector.tensor_copy(out=out_rounded[piece][:, :, t], in_=src)
+                elif t == PACK - 2 and piece == 0:
+                    nc.scalar.copy(out_rounded[piece][:, :, t : t + 2], src.unsqueeze(2).to_broadcast([P, U // 2, 2]))
                 else:
-                    nc.scalar.copy(out_rounded[q][:, :, t], src)
+                    nc.scalar.copy(out_rounded[piece][:, :, t], src)
 
         for t in range(PACK):
             copy_window(t)
@@ -219,63 +231,61 @@ def tile_picked_hashunderpaget_none_po_kernel(
         round_z(1, 0)
         fetch_diff(1, 1, 0)
         fetch_diff(1, 1, 1)
-        make_old_factor(0, 0)
+        for t in range(2):
+            make_tanh(h_bank[0, t], t, cols_of(0))
+        for t in range(2):
+            make_old_factor(t, cols_of(0))
+        make_new_part(h_bank[0, 0], 0, cols_of(0))
         for t in range(2, PACK):
             fetch_diff(1, t, 0)
             take_low(1, t - 1)
             round_z(1, t - 1)
             fetch_diff(1, t, 1)
-            if t == 2:
-                make_old_factor(0, 1)
         fetch_old(0, entries_of(n3_t, 0), cols_of(0))
         take_low(1, PACK - 1)
         round_z(1, PACK - 1)
         fetch_old(1, entries_of(n3_t, 0), cols_of(0))
-        new_first = [
-            keep.tile([P, HALF], F32, name="new_first0", align_bytes=64, tag="low1_3"),
-            keep.tile([P, HALF], F32, name="new_first1"),
-        ]
-        new_rest = [keep.tile([P, S], F32, name="new_rest%d" % t) for t in range(PACK)]
-        for t in range(2):
-            make_new_part(0, t, new_first[t][:])
-        for t in range(2, PACK):
-            make_old_factor(0, t)
-            make_new_part(0, t, new_rest[t][:, cols_of(0)])
+        put_new(0, entries_of(n3_t, 0), cols_of(0))
+        new_part[1] = keep.tile([P, S], F32, name="new_part1", align_bytes=64, tag="low1_3")
+        make_new_part(h_bank[0, 1], 1, cols_of(0))
         second_product(1)
+        put_new(1, entries_of(n3_t, 0), cols_of(0))
         for t in range(2):
-            put_new(t, entries_of(n3_t, 0), cols_of(0), new_first[t][:])
-        make_old_factor(1, 0)
-        make_old_factor(1, 1)
-        make_new_part(1, 0, new_rest[0][:, cols_of(1)])
-        make_old_factor(1, 2)
-        make_new_part(1, 1, new_rest[1][:, cols_of(1)])
-        make_old_factor(1, 3)
-        make_new_part(1, 2, new_rest[2][:, cols_of(1)])
-        make_new_part(1, 3, new_rest[3][:, cols_of(1)])
+            make_tanh(h_bank[1, t], t, cols_of(1))
+            make_old_factor(t, cols_of(1))
+        make_new_part(h_bank[1, 0], 0, cols_of(1))
+        make_tanh(h_bank[2], 2, slice(0, S))
+        make_new_part(h_bank[1, 1], 1, cols_of(1))
+        make_old_factor(2, slice(0, S))
+        make_tanh(h_bank[3], 3, slice(0, S))
+        make_new_part(h_bank[2], 2, slice(0, S))
+        make_old_factor(3, slice(0, S))
+        make_new_part(h_bank[3], 3, slice(0, S))
         fetch_old(0, entries_of(n3_t, 1), cols_of(1))
         fetch_old(1, entries_of(n3_t, 1), cols_of(1))
-        put_new(0, entries_of(n3_t, 1), cols_of(1), new_rest[0][:, cols_of(1)])
+        put_new(0, entries_of(n3_t, 1), cols_of(1))
         finish_tile(0)
         fetch_old(2, n3_t[:], slice(0, S))
-        put_new(1, entries_of(n3_t, 1), cols_of(1), new_rest[1][:, cols_of(1)])
+        put_new(1, entries_of(n3_t, 1), cols_of(1))
         finish_tile(1)
         fetch_old(3, n3_t[:], slice(0, S))
         for t in range(2, PACK):
-            put_new(t, n3_t[:], slice(0, S), new_rest[t][:])
+            put_new(t, n3_t[:], slice(0, S))
             finish_tile(t)
 
         out_scales = keep.tile([P, U], U8, align_bytes=64)
+        out_words = [keep.tile([P, U // 2], I32, name="out_words%d" % half, align_bytes=64) for half in range(2)]
         out_words_dram = words_view(out_1)
+        for piece in (1, 0, 2):
+            cols = PIECES[piece]
+            half, first = divmod(cols.start, U // 2)
+            nc.vector.quantize_mx(
+                out=out_words[half][:, first : first + cols.stop - cols.start].bitcast(FP8X4),
+                scales=out_scales[:, cols],
+                in_=out_rounded[piece][:].rearrange("p c t -> p (c t)"),
+            )
         for half in range(2):
-            out_words = keep.tile([P, 2 * QUARTER], I32, name="out_words%d" % half, align_bytes=64)
-            for i in range(2):
-                q = 2 * half + i
-                nc.vector.quantize_mx(
-                    out=out_words[:, i * QUARTER : (i + 1) * QUARTER].bitcast(FP8X4),
-                    scales=out_scales[:, q * QUARTER : (q + 1) * QUARTER],
-                    in_=out_rounded[q][:].rearrange("p c t -> p (c t)"),
-                )
-            nc.sync.dma_start(out_words_dram[:, 2 * half * QUARTER : 2 * (half + 1) * QUARTER], out_words[:])
+            nc.sync.dma_start(out_words_dram[:, half * U // 2 : (half + 1) * U // 2], out_words[half][:])
         scale_rows = out_2[0].rearrange("(q r) c -> r q c", r=PACK)
         for r in range(PACK):
             engine = nc.scalar if r % 2 else nc.sync

@@ -71,8 +71,6 @@ def tile_picked_hashunderpaget_none_po_kernel(
         n1_t = load_list(n1, "n1_t")
         n2_t = load_list(n2, "n2_t")
         n3_t = load_list(n3, "n3_t")
-        w2_raw = keep.tile([P, N], I32, align_bytes=64, tag="w2_raw")
-        nc.sync.dma_start(w2_raw[:], words_view(w2_words))
 
         gain = keep.tile([P, PACK], F32)
         nc.gpsimd.dma_start(gain[:], gn.rearrange("(p t) o -> p (t o)", t=PACK))
@@ -88,8 +86,10 @@ def tile_picked_hashunderpaget_none_po_kernel(
         for r in range(1, PACK):
             nc.scalar.dma_start(xs_plane[r:P:32, :].bitcast(I32), xs_picked[8 * r : P : 32, :].bitcast(I32))
         w1_dealt = deal(w1_raw, I32, "w1_dealt", "slot1")
-        w2s_raw = load_weight_scales(w2_scales, "w2s_raw", "w1_raw")
+        w2_raw = keep.tile([P, N], I32, align_bytes=64, tag="w1_raw")
+        nc.sync.dma_start(w2_raw[:], words_view(w2_words))
         w1s_dealt = deal(w1s_raw, U8, "w1s_dealt", "w1s_dealt")
+        w2s_raw = load_weight_scales(w2_scales, "w2s_raw", "w1s_raw")
         xw_picked = []
         for c in range(2):
             xw_picked.append(keep.tile([P, HALF], U32, name="xw_picked%d" % c, align_bytes=64, tag="slot%d" % (2 + c)))
@@ -218,11 +218,11 @@ def tile_picked_hashunderpaget_none_po_kernel(
             take_low(0, t - 1)
             round_z(0, t - 1)
             fetch_diff(0, t, 1)
-        w2s_dealt = deal(w2s_raw, U8, "w2s_dealt", "low0_1")
         fetch_diff(1, 0, 0)
         take_low(0, PACK - 1)
         round_z(0, PACK - 1)
         fetch_diff(1, 0, 1)
+        w2s_dealt = deal(w2s_raw, U8, "w2s_dealt", "low0_2")
         copy_plain(1, 1, "low0_3")
         copy_plain(1, 2, "y_plain1_2")
         copy_plain(1, 3, "y_plain1_3")
@@ -274,19 +274,22 @@ def tile_picked_hashunderpaget_none_po_kernel(
             finish_tile(t)
 
         out_scales = keep.tile([P, U], U8, align_bytes=64)
-        out_words = [keep.tile([P, U // 2], I32, name="out_words%d" % half, align_bytes=64) for half in range(2)]
         out_words_dram = words_view(out_1)
-        for piece in (1, 0, 2):
+
+        def quantise_piece(piece):
             cols = PIECES[piece]
-            half, first = divmod(cols.start, U // 2)
+            out_words = keep.tile([P, cols.stop - cols.start], I32, name="out_words%d" % piece, align_bytes=64)
             nc.vector.quantize_mx(
-                out=out_words[half][:, first : first + cols.stop - cols.start].bitcast(FP8X4),
+                out=out_words[:].bitcast(FP8X4),
                 scales=out_scales[:, cols],
                 in_=out_rounded[piece][:].rearrange("p c t -> p (c t)"),
             )
-        for half in range(2):
-            nc.sync.dma_start(out_words_dram[:, half * U // 2 : (half + 1) * U // 2], out_words[half][:])
+            return out_words
+
+        for piece in (1, 0):
+            nc.sync.dma_start(out_words_dram[:, PIECES[piece]], quantise_piece(piece)[:])
+        last_words = quantise_piece(2)
         scale_rows = out_2[0].rearrange("(q r) c -> r q c", r=PACK)
         for r in range(PACK):
-            engine = nc.scalar if r % 2 else nc.sync
-            engine.dma_start(scale_rows[r].bitcast(I32), out_scales[r:P:32, :].bitcast(I32))
+            (nc.sync if r % 2 else nc.scalar).dma_start(scale_rows[r].bitcast(I32), out_scales[r:P:32, :].bitcast(I32))
+        nc.scalar.dma_start(out_words_dram[:, PIECES[2]], last_words[:])

@@ -74,10 +74,6 @@ def tile_picked_hashunderpaget_none_po_kernel(
 
         gain = keep.tile([P, PACK], F32)
         nc.gpsimd.dma_start(gain[:], gn.rearrange("(p t) o -> p (t o)", t=PACK))
-        warm = keep.tile([P, 1], F32)
-        nc.vector.memset(warm[:], 0.0)
-        warm_out = keep.tile([P, 1], F32)
-        nc.scalar.activation(warm_out[:], warm[:], ACT.Silu)
 
         xs_picked = keep.tile([P, S], U8, align_bytes=64, tag="slot0")
         nc.vector.tensor_copy(out=xs_picked[:], in_=xs_all[:].indirect(offs_t[:]))

from contextlib import ExitStack

import concourse.mybir as mybir

K, T, S, N, H, U = 512, 2048, 512, 512, 512, 1024
FLOPS = 2 * K * H * S + 2 * H * N * S

F32 = mybir.dt.float32
BF16 = mybir.dt.bfloat16
I32 = mybir.dt.int32
U32 = mybir.dt.uint32
U16 = mybir.dt.uint16
U8 = mybir.dt.uint8
FP8X4 = mybir.dt.float8_e4m3fn_x4
ACT = mybir.ActivationFunctionType
ALU = mybir.AluOpType

P = 128
PACK = 4
HALF = S // 2
LIST_COLS = S // 16
PIECES = (slice(0, U // 2), slice(U // 2, 3 * U // 4), slice(3 * U // 4, U))


def tile_picked_hashunderpaget_none_po_kernel(
    tc, x_words, x_scales, w1_words, w1_scales, gn, w2_words, w2_scales, mem, offs, n1, n2, n3, out_0, out_1, out_2
):
    nc = tc.nc
    with ExitStack() as ctx:
        lists = ctx.enter_context(tc.tile_pool(name="lists", bufs=1))
        keep = ctx.enter_context(tc.tile_pool(name="keep", bufs=1))
        ring = ctx.enter_context(tc.tile_pool(name="ring", bufs=3))
        psum = ctx.enter_context(tc.psum_pool(name="psum", bufs=1))

        def words_view(words):
            return words[0].rearrange("p c r -> p (c r)").bitcast(I32)

        def load_list(src, name):
            tile = lists.tile([P, LIST_COLS], U16, name=name)
            nc.sync.dma_start(tile[:], src)
            return tile

        def entries_of(list_tile, c):
            return list_tile[:, c * LIST_COLS // 2 : (c + 1) * LIST_COLS // 2]

        def cols_of(c):
            return slice(c * HALF, (c + 1) * HALF)

        def load_weight_scales(scales, name, tag):
            raw = keep.tile([P, H], U8, name=name, align_bytes=64, tag=tag)
            rows = scales[0].bitcast(I32).rearrange("(q r) c -> r q c", r=PACK)
            for r in range(PACK):
                nc.sync.dma_start(raw[r:P:PACK, :].bitcast(I32), rows[r].unsqueeze(1).to_broadcast([4, 8, H // 4]))
            return raw

        def deal(raw, dtype, name, tag):
            dealt = keep.tile([P, PACK, P], dtype, name=name, align_bytes=64, tag=tag)
            nc.vector.tensor_copy(
                out=dealt[:].rearrange("p t m -> p m t"), in_=raw[:].rearrange("p (m t) -> p m t", t=PACK)
            )
            return dealt

        offs_t = load_list(offs, "offs_t")
        xs_all = keep.tile([P, T], U8, align_bytes=64)
        nc.sync.dma_start(xs_all[:].bitcast(I32), x_scales[0].bitcast(I32).unsqueeze(1).to_broadcast([16, 8, T // 4]))
        w1s_raw = load_weight_scales(w1_scales, "w1s_raw", "w1s_raw")
        w1_raw = keep.tile([P, H], I32, align_bytes=64, tag="w1_raw")
        nc.sync.dma_start(w1_raw[:], words_view(w1_words))
        xw_all = keep.tile([P, T], I32, align_bytes=64, tag="xw_all")
        nc.sync.dma_start(xw_all[:], words_view(x_words))
        n1_t = load_list(n1, "n1_t")
        n2_t = load_list(n2, "n2_t")
        n3_t = load_list(n3, "n3_t")

        gain = keep.tile([P, PACK], F32)
        nc.gpsimd.dma_start(gain[:], gn.rearrange("(p t) o -> p (t o)", t=PACK))

        xs_picked = keep.tile([P, S], U8, align_bytes=64, tag="slot0")
        nc.vector.tensor_copy(out=xs_picked[:], in_=xs_all[:].indirect(offs_t[:]))
        xs_plane = keep.tile([P, S], U8, align_bytes=64)
        nc.vector.tensor_copy(out=xs_plane[:].bitcast(I32), in_=xs_picked[:].bitcast(I32))
        for r in range(1, PACK):
            nc.scalar.dma_start(xs_plane[r:P:32, :].bitcast(I32), xs_picked[8 * r : P : 32, :].bitcast(I32))
        w1_dealt = deal(w1_raw, I32, "w1_dealt", "slot1")
        w2_raw = keep.tile([P, N], I32, align_bytes=64, tag="w1_raw")
        nc.sync.dma_start(w2_raw[:], words_view(w2_words))
        w1s_dealt = deal(w1s_raw, U8, "w1s_dealt", "w1s_dealt")
        w2s_raw = load_weight_scales(w2_scales, "w2s_raw", "w1s_raw")
        xw_picked = []
        for c in range(2):
            xw_picked.append(keep.tile([P, HALF], U32, name="xw_picked%d" % c, align_bytes=64, tag="slot%d" % (2 + c)))
            nc.vector.tensor_copy(out=xw_picked[c][:], in_=xw_all[:].bitcast(U32).indirect(entries_of(offs_t, c)))

        y_bank = {}
        for t in range(PACK):
            for c in range(2):
                y_bank[c, t] = psum.tile([P, HALF], F32, name="y_bank%d_%d" % (c, t), tag="bank%d" % (PACK * c + t))
                nc.tensor.matmul_mx(
                    out=y_bank[c, t][:],
                    lhsT=w1_dealt[:, t, :].bitcast(FP8X4),
                    lhsT_scale=w1s_dealt[:, t, :],
                    rhs=xw_picked[c][:].bitcast(FP8X4),
                    rhs_scale=xs_plane[:, cols_of(c)],
                    start=True,
                    stop=True,
                )
        w2_dealt = deal(w2_raw, I32, "w2_dealt", "xw_all")

        mem_rows = mem.rearrange("(p t) u -> t p u", t=PACK)
        page = []
        for t in range(PACK):
            page.append(keep.tile([P, U], F32, name="page%d" % t, align_bytes=64, tag="slot%d" % t))
            nc.sync.dma_start(page[t][:], mem_rows[t])

        y_window = [keep.tile([P, S], F32, name="y_window%d" % t) for t in range(PACK)]
        z_rounded = [keep.tile([P, HALF, PACK], BF16, name="z_rounded%d" % c, align_bytes=64) for c in range(2)]
        y_plain, diffs, low, h_bank = {}, {}, {}, {}

        def copy_window(t):
            for c in range(2):
                if (c, t) == (1, 0):
                    nc.vector.tensor_scalar_mul(y_window[t][:, cols_of(c)], y_bank[c, t][:], -1.0)
                else:
                    nc.scalar.activation(y_window[t][:, cols_of(c)], y_bank[c, t][:], ACT.Copy, scale=-1.0)

        def copy_plain(c, t, tag):
            y_plain[c, t] = keep.tile([P, HALF], F32, name="y_plain%d_%d" % (c, t), align_bytes=64, tag=tag)
            nc.scalar.activation(y_plain[c, t][:], y_bank[c, t][:], ACT.Copy, scale=-1.0)

        def fetch_diff(c, t, which):
            diffs[c, t, which] = ring.tile([P, HALF], F32, name="diff%d" % which)
            entries = entries_of((n1_t, n2_t)[which], c)
            nc.vector.tensor_tensor(diffs[c, t, which][:], y_window[t][:].indirect(entries), y_plain[c, t][:], ALU.subtract)

        def take_low(c, t):
            low[c, t] = keep.tile([P, HALF], F32, name="low%d_%d" % (c, t), align_bytes=64, tag="low%d_%d" % (c, t))
            nc.vector.tensor_tensor(low[c, t][:], diffs[c, t, 0][:], diffs[c, t, 1][:], ALU.max)

        def round_z(c, t):
            nc.scalar.activation(z_rounded[c][:, :, t], low[c, t][:], ACT.Copy, scale=gain[:, t : t + 1])

        def second_product(c):
            z_words = keep.tile([P, HALF], U32, name="z_words%d" % c, align_bytes=64)
            z_scales = keep.tile([P, HALF], U8, name="z_scales%d" % c, align_bytes=64)
            nc.vector.quantize_mx(
                out=z_words[:].bitcast(FP8X4), scales=z_scales[:], in_=z_rounded[c][:].rearrange("p j t -> p (j t)")
            )
            for t in range(PACK):
                if t < 2:
                    h_bank[c, t] = psum.tile([P, HALF], F32, name="h_bank%d_%d" % (c, t), tag="bank%d" % (PACK * c + t))
                    h_half = h_bank[c, t][:]
                else:
                    if c == 0:
                        h_bank[t] = psum.tile([P, S], F32, name="h_bank%d" % t, tag="bank%d" % t)
                    h_half = h_bank[t][:, cols_of(c)]
                nc.tensor.matmul_mx(
                    out=h_half,
                    lhsT=w2_dealt[:, t, :].bitcast(FP8X4),
                    lhsT_scale=w2s_dealt[:, t, :],
                    rhs=z_words[:].bitcast(FP8X4),
                    rhs_scale=z_scales[:],
                    start=True,
                    stop=True,
                )

        old_factor = [keep.tile([P, S], F32, name="old_factor%d" % t) for t in range(PACK)]
        old_part = [keep.tile([P, S], F32, name="old_part%d" % t) for t in range(PACK)]

        tanh_half = [keep.tile([P, S], F32, name="tanh_half%d" % t) for t in range(PACK)]

        new_part = {t: keep.tile([P, S], F32, name="new_part%d" % t) for t in (0, 2, 3)}

        def make_tanh(bank, t, cols):
            nc.scalar.activation(tanh_half[t][:, cols], bank[:], ACT.Tanh, scale=0.5)

        def make_old_factor(t, cols):
            nc.scalar.activation(old_factor[t][:, cols], tanh_half[t][:, cols], ACT.Copy, scale=-0.5, bias=0.5)

        def make_new_part(bank, t, cols):
            nc.scalar.activation(new_part[t][:, cols], bank[:], ACT.Silu)

        def fetch_old(t, entries, cols):
            nc.vector.tensor_tensor(old_part[t][:, cols], page[t][:].indirect(entries), old_factor[t][:, cols], ALU.mult)

        def put_new(t, entries, cols):
            nc.vector.tensor_tensor(page[t][:].indirect(entries), old_part[t][:, cols], new_part[t][:, cols], ALU.add)

        out_rows = out_0.rearrange("(p t) u -> t p u", t=PACK)
        out_rounded = [
            keep.tile([P, cols.stop - cols.start, PACK], BF16, name="out_rounded%d" % piece, align_bytes=64)
            for piece, cols in enumerate(PIECES)
        ]

        def finish_tile(t):
            nc.sync.dma_start(out_rows[t], page[t][:])
            for piece, cols in enumerate(PIECES):
                src = page[t][:, cols]
                if t == PACK - 1 and piece == 0:
                    nc.vector.tensor_copy(out=out_rounded[piece][:, :, t], in_=src)
                elif t == PACK - 2 and piece == 0:
                    nc.scalar.copy(out_rounded[piece][:, :, t : t + 2], src.unsqueeze(2).to_broadcast([P, U // 2, 2]))
                else:
                    nc.scalar.copy(out_rounded[piece][:, :, t], src)

        for t in range(PACK):
            copy_window(t)
            copy_plain(0, t, "y_plain0_%d" % t)
        copy_plain(1, 0, "y_plain1_0")

        fetch_diff(0, 0, 0)
        fetch_diff(0, 0, 1)
        for t in range(1, PACK):
            fetch_diff(0, t, 0)
            take_low(0, t - 1)
            round_z(0, t - 1)
            fetch_diff(0, t, 1)
        fetch_diff(1, 0, 0)
        take_low(0, PACK - 1)
        round_z(0, PACK - 1)
        fetch_diff(1, 0, 1)
        w2s_dealt = deal(w2s_raw, U8, "w2s_dealt", "low0_2")
        copy_plain(1, 1, "low0_3")
        copy_plain(1, 2, "y_plain1_2")
        copy_plain(1, 3, "y_plain1_3")
        take_low(1, 0)
        second_product(0)
        round_z(1, 0)
        fetch_diff(1, 1, 0)
        fetch_diff(1, 1, 1)
        for t in range(2):
            make_tanh(h_bank[0, t], t, cols_of(0))
        for t in range(2):
            make_old_factor(t, cols_of(0))
        make_new_part(h_bank[0, 0], 0, cols_of(0))
        for t in range(2, PACK):
            fetch_diff(1, t, 0)
            take_low(1, t - 1)
            round_z(1, t - 1)
            fetch_diff(1, t, 1)
        fetch_old(0, entries_of(n3_t, 0), cols_of(0))
        take_low(1, PACK - 1)
        round_z(1, PACK - 1)
        fetch_old(1, entries_of(n3_t, 0), cols_of(0))
        put_new(0, entries_of(n3_t, 0), cols_of(0))
        new_part[1] = keep.tile([P, S], F32, name="new_part1", align_bytes=64, tag="low1_3")
        make_new_part(h_bank[0, 1], 1, cols_of(0))
        second_product(1)
        put_new(1, entries_of(n3_t, 0), cols_of(0))
        for t in range(2):
            make_tanh(h_bank[1, t], t, cols_of(1))
            make_old_factor(t, cols_of(1))
        make_new_part(h_bank[1, 0], 0, cols_of(1))
        make_tanh(h_bank[2], 2, slice(0, S))
        make_new_part(h_bank[1, 1], 1, cols_of(1))
        make_old_factor(2, slice(0, S))
        make_tanh(h_bank[3], 3, slice(0, S))
        make_new_part(h_bank[2], 2, slice(0, S))
        make_old_factor(3, slice(0, S))
        make_new_part(h_bank[3], 3, slice(0, S))
        fetch_old(0, entries_of(n3_t, 1), cols_of(1))
        fetch_old(1, entries_of(n3_t, 1), cols_of(1))
        put_new(0, entries_of(n3_t, 1), cols_of(1))
        finish_tile(0)
        fetch_old(2, n3_t[:], slice(0, S))
        put_new(1, entries_of(n3_t, 1), cols_of(1))
        finish_tile(1)
        fetch_old(3, n3_t[:], slice(0, S))
        for t in range(2, PACK):
            put_new(t, n3_t[:], slice(0, S))
            finish_tile(t)

        out_scales = keep.tile([P, U], U8, align_bytes=64)
        out_words_dram = words_view(out_1)

        def quantise_piece(piece):
            cols = PIECES[piece]
            out_words = keep.tile([P, cols.stop - cols.start], I32, name="out_words%d" % piece, align_bytes=64)
            nc.vector.quantize_mx(
                out=out_words[:].bitcast(FP8X4),
                scales=out_scales[:, cols],
                in_=out_rounded[piece][:].rearrange("p c t -> p (c t)"),
            )
            return out_words

        for piece in (1, 0):
            nc.sync.dma_start(out_words_dram[:, PIECES[piece]], quantise_piece(piece)[:])
        last_words = quantise_piece(2)
        scale_rows = out_2[0].rearrange("(q r) c -> r q c", r=PACK)
        for r in range(PACK):
            (nc.sync if r % 2 else nc.scalar).dma_start(scale_rows[r].bitcast(I32), out_scales[r:P:32, :].bitcast(I32))
        nc.scalar.dma_start(out_words_dram[:, PIECES[2]], last_words[:])
